import numpy as np
import ml_dtypes


def mxq(x, axis, fmt="e4m3"):
    dtype, down = {"e4m3": (ml_dtypes.float8_e4m3fn, 7), "e5m2": (ml_dtypes.float8_e5m2, 14)}[fmt]
    v = np.moveaxis(np.asarray(x, np.float32).astype(ml_dtypes.bfloat16).astype(np.float64), axis, -1)
    blocks = v.reshape(v.shape[:-1] + (-1, 32))
    amax = np.abs(blocks).max(-1, keepdims=True)
    byte = np.maximum(np.where(amax > 0, np.frexp(amax)[1] - 1 + 127, 0) - down, 1)
    scale = np.exp2(byte - 127.0)
    codes = (blocks / scale).astype(np.float32).astype(dtype).astype(np.float64)
    return np.moveaxis((codes * scale).reshape(v.shape), -1, axis)


WIDE = False


def mx_kscale(k):
    if not WIDE:
        return np.ones(k)
    levels = np.array([10, -10, 5, -5, 0])
    if k % 512:
        return np.exp2(np.random.permutation(np.resize(levels, k // 32))).repeat(32)
    a = np.empty((k // 512, 16))
    for p in range(k // 512):
        a[p, :8] = np.random.permutation(np.resize(levels, 8))
        for g in range(8):
            far = levels[np.abs(levels - a[p, g]) >= 10]
            a[p, g + 8] = far[np.random.randint(len(far))]
    return np.exp2(a.ravel()).repeat(32)


def f64(x):
    return np.asarray(x).astype(np.float64)


def striped(idx):
    return np.tile(idx.reshape(-1, 16).T, (8, 1)).astype(np.uint16)


def unstriped(offs):
    return offs[:16].T.reshape(-1).astype(np.int64)


E2M1 = np.array([0.0, 0.5, 1.0, 1.5, 2.0, 3.0, 4.0, 6.0, -0.0, -0.5, -1.0, -1.5, -2.0, -3.0, -4.0, -6.0])


def pack_weight(w, fmt):
    k, n = w.shape
    w = f64(np.asarray(w, np.float32).astype(ml_dtypes.bfloat16)).reshape(k // 32, 32, n)
    amax = np.abs(w).max(1)
    if fmt == "e4m3":
        byte = np.frexp(amax)[1] - 1 + 127 - 7
    else:
        mant, ex = np.frexp(amax / 6.0)
        byte = np.where(mant > 0.5, ex, ex - 1) + 127
    byte = np.clip(np.where(amax > 0, byte, 1), 1, 254)
    scaled = (w * np.exp2(127.0 - byte)[:, None, :]).reshape(k, n).astype(np.float32)
    by_word = np.ascontiguousarray(scaled.reshape(k // 512, 128, 4, n).transpose(0, 1, 3, 2))
    if fmt == "e4m3":
        words = by_word.astype(ml_dtypes.float8_e4m3fn).view(np.uint8)
    else:
        c = by_word.astype(ml_dtypes.float4_e2m1fn).view(np.uint8) & 0xF
        words = (c[..., 0::2] | (c[..., 1::2] << 4)).reshape(k // 512, 128, 2 * n)
    return np.ascontiguousarray(words), np.ascontiguousarray(byte.astype(np.uint8).reshape(k // 512, 16, n))


def unpack_weight(words, scales, fmt):
    g, _, n = scales.shape
    words = np.ascontiguousarray(words).reshape(g, 128, n, -1)
    if fmt == "e4m3":
        vals = words.view(ml_dtypes.float8_e4m3fn).astype(np.float64)
    else:
        nib = np.empty((g, 128, n, 4), np.uint8)
        nib[..., 0::2] = words & 0xF
        nib[..., 1::2] = words >> 4
        vals = E2M1[nib]
    vals = vals * np.repeat(np.exp2(scales.astype(np.float64) - 127.0), 8, axis=1)[..., None]
    return vals.transpose(0, 1, 3, 2).reshape(g * 512, n)


def gelu(v):
    return 0.5 * v * (1.0 + np.tanh(np.sqrt(2.0 / np.pi) * (v + 0.044715 * v**3)))


K, H, T, T3, S, S2 = 1536, 1024, 2048, 2048, 512, 512

def setup_inputs():
    n = np.random.standard_normal
    s = mx_kscale(K)[:, None]
    u = mx_kscale(H)[:, None]
    tab_words, tab_scales = pack_weight(n((K, T)) * s, "e4m3")
    tab2_words, tab2_scales = pack_weight(n((H, T3)) / np.sqrt(H) / u, "e4m3")
    tab3_words, tab3_scales = pack_weight(n((H, T3)) / np.sqrt(H) / u, "e4m3")
    w4_words, w4_scales = pack_weight(1.6 * n((K, H)) / np.sqrt(K) / s, "e2m1")
    return {
        "tab_words": tab_words, "tab_scales": tab_scales,
        "offs": striped(np.random.permutation(T)[:S]),
        "tab2_words": tab2_words, "tab2_scales": tab2_scales,
        "offs2": striped(np.random.permutation(T3)[:S2]),
        "tab3_words": tab3_words, "tab3_scales": tab3_scales,
        "offs3": striped(np.random.permutation(T3)[:S2]),
        "w1": (n((K, H)) / np.sqrt(K) / s).astype(np.float32),
        "w4_words": w4_words, "w4_scales": w4_scales,
        "b4": (0.5 * n(H)).astype(np.float32),
        "gain": (np.exp(0.3 * n(H)) * u[:, 0]).astype(np.float32),
        "cap": (0.3 + 0.8 * n((S2, S))).astype(np.float32),
    }

def reference(tab_words, tab_scales, offs, tab2_words, tab2_scales, offs2, tab3_words, tab3_scales, offs3,
              w1, w4_words, w4_scales, b4, gain, cap):
    v = unpack_weight(tab_words, tab_scales, "e4m3")[:, unstriped(offs)]
    v2 = unpack_weight(tab2_words, tab2_scales, "e4m3")[:, unstriped(offs2)]
    v3 = unpack_weight(tab3_words, tab3_scales, "e4m3")[:, unstriped(offs3)]
    w4 = unpack_weight(w4_words, w4_scales, "e2m1")
    direct = mxq(f64(w1), 0, "e4m3").T @ v
    bent = np.tanh((w4.T @ v) + f64(b4)[:, None])
    h = np.maximum(direct, bent) * f64(gain)[:, None]
    hq = mxq(h, 0, "e4m3")
    e2 = v2.T @ hq
    e3 = v3.T @ hq
    return np.minimum(e2, f64(cap)) + e3

@@ -1,0 +1,269 @@
+from contextlib import ExitStack
+
+import concourse.mybir as mybir
+
+K, H, T, S = 1536, 1024, 2048, 512
+FLOPS = 2 * (2 * K * H * S + 2 * H * S * S)
+
+F32 = mybir.dt.float32
+BF16 = mybir.dt.bfloat16
+I32 = mybir.dt.int32
+U32 = mybir.dt.uint32
+U16 = mybir.dt.uint16
+U8 = mybir.dt.uint8
+FP8X4 = mybir.dt.float8_e4m3fn_x4
+FP4X4 = mybir.dt.float4_e2m1fn_x4
+ALU = mybir.AluOpType
+ACT = mybir.ActivationFunctionType
+
+P = 128
+PACK = 4
+KP = P * PACK
+K_PASSES = K // KP
+R_PASSES = H // KP
+M_TILES = S // P
+LIST_COLS = S // 16
+CAND_ROW = (4, 8)
+
+
+def tile_list_graft_sharing_score_kernel(
+    tc, tab_words, tab_scales, offs, tab2_words, tab2_scales, offs2, tab3_words, tab3_scales, offs3,
+    w1, w4_words, w4_scales, b4, gain, cap, out,
+):
+    nc = tc.nc
+    with ExitStack() as ctx:
+        keep = ctx.enter_context(tc.tile_pool(name="keep", bufs=1))
+        ring = ctx.enter_context(tc.tile_pool(name="ring", bufs=3))
+        stream = ctx.enter_context(tc.tile_pool(name="stream", bufs=5))
+        psum = ctx.enter_context(tc.psum_pool(name="psum", bufs=1))
+
+        def held(name, shape, dtype):
+            return keep.tile(shape, dtype, name=name, align_bytes=64)
+
+        def staged(name, shape, dtype):
+            return stream.tile(shape, dtype, name=name, tag="staged", align_bytes=64)
+
+        def bank(n, name):
+            return psum.tile([P, S], F32, name=name, tag="bank%d" % n)
+
+        lists = [held("list%d" % n, [P, LIST_COLS], U16) for n in range(3)]
+
+        tab_sc = staged("tab_sc", [P, K_PASSES, T], U8)
+        w4_sc_raw = staged("w4_sc_raw", [P, K_PASSES, H], U8)
+        cand_sc = [held("cand_sc%d" % n, [P, T], U8) for n in range(2)]
+        nc.vector.memset(tab_sc[:].bitcast(I32), 0)
+        for n in range(2):
+            nc.gpsimd.memset(cand_sc[n][:].bitcast(I32), 0)
+        nc.vector.memset(w4_sc_raw[:].bitcast(I32), 0)
+
+        def load_planes(dst, src):
+            for q in range(4):
+                nc.sync.dma_start(
+                    out=dst[32 * q : 32 * q + 4, :, :].bitcast(I32),
+                    in_=src[:, 4 * q : 4 * q + 4, :].rearrange("a r t -> r a t").bitcast(I32),
+                )
+
+        def load_packed(n, src):
+            for q in range(4):
+                first = 32 * q + CAND_ROW[n]
+                nc.gpsimd.dma_start(
+                    out=cand_sc[n][first : first + 4 * R_PASSES, :].bitcast(I32),
+                    in_=src[:, 4 * q : 4 * q + 4, :].bitcast(I32),
+                )
+
+        load_packed(0, tab2_scales)
+        load_packed(1, tab3_scales)
+
+        w4_raw = [staged("w4_raw%d" % a, [P, 2 * H], U8) for a in range(K_PASSES)]
+        w1_raw = {}
+        tab_w = []
+        cand_w = {}
+
+        def load_w1(a, b):
+            w1_raw[a, b] = staged("w1_raw%d%d" % (a, b), [P, PACK, KP], F32)
+            nc.sync.dma_start(
+                out=w1_raw[a, b][:],
+                in_=w1[a * KP : (a + 1) * KP, b * KP : (b + 1) * KP].rearrange("(p j) c -> p j c", j=PACK),
+            )
+
+        def load_words(name, src):
+            words = staged(name, [P, T], I32)
+            nc.sync.dma_start(out=words[:], in_=src.rearrange("p t i -> p (t i)").bitcast(I32))
+            return words
+
+        for n, src in enumerate((offs, offs2, offs3)):
+            nc.sync.dma_start(lists[n][:], src)
+        bias = held("bias", [P, R_PASSES, PACK], F32)
+        gains = held("gains", [P, R_PASSES, PACK], F32)
+        nc.gpsimd.dma_start(out=bias[:], in_=b4.rearrange("(b p t) -> p b t", p=P, t=PACK))
+        nc.gpsimd.dma_start(out=gains[:], in_=gain.rearrange("(b p t) -> p b t", p=P, t=PACK))
+        for a in range(K_PASSES):
+            nc.sync.dma_start(out=w4_raw[a][:].bitcast(I32), in_=w4_words[a].bitcast(I32))
+        load_planes(tab_sc, tab_scales)
+        load_planes(w4_sc_raw, w4_scales)
+        for a in range(K_PASSES):
+            load_w1(a, 0)
+            tab_w.append(load_words("tab_w%d" % a, tab_words[a]))
+        load_w1(0, 1)
+        load_w1(1, 1)
+        cand_w[0, 0] = load_words("cand_w00", tab2_words[0])
+        load_w1(2, 1)
+        cand_w[0, 1] = load_words("cand_w01", tab2_words[1])
+        cand_w[1, 0] = load_words("cand_w10", tab3_words[0])
+        cap_sb = staged("cap_sb", [P, M_TILES, S], F32)
+        nc.sync.dma_start(out=cap_sb[:], in_=cap.rearrange("(i p) j -> p i j", p=P))
+        cand_w[1, 1] = load_words("cand_w11", tab3_words[1])
+
+        w4_codes = held("w4_codes", [P, K_PASSES, 2 * H], U8)
+        w4_sc = held("w4_sc", [P, K_PASSES, H], U8)
+        for a in range(K_PASSES):
+            nc.scalar.copy(
+                out=w4_codes[:, a, :].bitcast(U16).rearrange("p (b t m) -> p b t m", b=R_PASSES, t=PACK),
+                in_=w4_raw[a][:].bitcast(U16).rearrange("p (b m t) -> p b t m", b=R_PASSES, t=PACK),
+            )
+
+        v_codes = held("v_codes", [P, K_PASSES, S], U32)
+        v_sc = held("v_sc", [P, K_PASSES, S], U8)
+        for a in range(K_PASSES):
+            nc.vector.tensor_copy(v_sc[:, a, :], tab_sc[:, a, :].indirect(lists[0][:]))
+        for a in range(K_PASSES):
+            nc.vector.tensor_copy(
+                out=w4_sc[:, a, :].rearrange("p (b t m) -> p b t m", b=R_PASSES, t=PACK),
+                in_=w4_sc_raw[:, a, :].rearrange("p (b m t) -> p b t m", b=R_PASSES, t=PACK),
+            )
+
+        w1_codes = {}
+        w1_sc = {}
+
+        def quantize_w1(a, b):
+            grouped = ring.tile([P, PACK, P, PACK], BF16, name="w1_grouped", align_bytes=64)
+            nc.scalar.copy(
+                out=grouped[:].rearrange("p t m j -> p m j t"),
+                in_=w1_raw[a, b][:].rearrange("p j (m t) -> p m j t", t=PACK),
+            )
+            w1_codes[a, b] = held("w1_codes%d%d" % (a, b), [P, KP], U32)
+            w1_sc[a, b] = held("w1_sc%d%d" % (a, b), [P, KP], U8)
+            nc.vector.quantize_mx(
+                out=w1_codes[a, b][:].bitcast(FP8X4),
+                scales=w1_sc[a, b][:],
+                in_=grouped[:].rearrange("p t m j -> p (t m j)"),
+            )
+
+        def bent_pass(acc, a, b):
+            for t in range(PACK):
+                c0 = b * KP + t * P
+                nc.tensor.matmul_mx(
+                    out=acc[t][:],
+                    lhsT=w4_codes[:, a, 2 * c0 : 2 * (c0 + P)].bitcast(FP4X4),
+                    lhsT_scale=w4_sc[:, a, c0 : c0 + P],
+                    rhs=v_codes[:, a, :].bitcast(FP8X4),
+                    rhs_scale=v_sc[:, a, :],
+                    start=(a == 0),
+                    stop=(a == K_PASSES - 1),
+                )
+
+        def direct_pass(acc, a, b):
+            for t in range(PACK):
+                cols = slice(t * P, (t + 1) * P)
+                nc.tensor.matmul_mx(
+                    out=acc[t][:],
+                    lhsT=w1_codes[a, b][:, cols].bitcast(FP8X4),
+                    lhsT_scale=w1_sc[a, b][:, cols],
+                    rhs=v_codes[:, a, :].bitcast(FP8X4),
+                    rhs_scale=v_sc[:, a, :],
+                    start=(a == 0),
+                    stop=(a == K_PASSES - 1),
+                )
+
+        def tanh_out(acc, b):
+            bent = []
+            for t in range(PACK):
+                bent.append(keep.tile([P, S], F32, name="bent%d%d" % (b, t), tag="bent%d" % t, align_bytes=64))
+                nc.scalar.activation(out=bent[t][:], in_=acc[t][:], func=ACT.Tanh, bias=bias[:, b, t : t + 1])
+            return bent
+
+        h_codes = []
+        h_sc = []
+
+        def make_h(direct, bent, b):
+            rows = keep.tile([P, PACK, S], BF16, name="h_rows%d" % b, tag="h_rows", align_bytes=64)
+            for t in range(PACK):
+                nc.vector.tensor_tensor(out=bent[t][:], in0=direct[t][:], in1=bent[t][:], op=ALU.max)
+                nc.scalar.activation(out=rows[:, t, :], in_=bent[t][:], func=ACT.Copy, scale=gains[:, b, t : t + 1])
+            grouped = keep.tile([P, S, PACK], BF16, name="h_grouped%d" % b, tag="h_grouped", align_bytes=64)
+            nc.vector.tensor_copy(
+                out=grouped[:].rearrange("p (c i) t -> p c t i", i=4),
+                in_=rows[:].rearrange("p t (c i) -> p c t i", i=4),
+            )
+            h_codes.append(held("h_codes%d" % b, [P, S], U32))
+            h_sc.append(held("h_sc%d" % b, [P, S], U8))
+            nc.vector.quantize_mx(
+                out=h_codes[b][:].bitcast(FP8X4), scales=h_sc[b][:], in_=grouped[:].rearrange("p j t -> p (j t)")
+            )
+
+        cand_codes = {}
+        cand_planes = [held("cand_planes%d" % n, [P, S], U8) for n in range(2)]
+
+        def gather_cand(n, b, pieces):
+            cand_codes[n, b] = held("cand_codes%d%d" % (n, b), [P, S], U32)
+            width = S // pieces
+            for u in range(pieces):
+                nc.vector.tensor_copy(
+                    cand_codes[n, b][:, u * width : (u + 1) * width],
+                    cand_w[n, b][:].bitcast(U32).indirect(lists[1 + n][:, u * width // 16 : (u + 1) * width // 16]),
+                )
+
+        def score_pass(acc, n, b, i):
+            cols = slice(i * P, (i + 1) * P)
+            nc.tensor.matmul_mx(
+                out=acc[:],
+                lhsT=cand_codes[n, b][:, cols].bitcast(FP8X4),
+                lhsT_scale=cand_planes[n][CAND_ROW[n] + 4 * b :, cols],
+                rhs=h_codes[b][:].bitcast(FP8X4),
+                rhs_scale=h_sc[b][:],
+                start=(b == 0),
+                stop=(b == R_PASSES - 1),
+            )
+
+        direct = [bank(t, "direct0%d" % t) for t in range(PACK)]
+        curved = [bank(PACK + t, "curved0%d" % t) for t in range(PACK)]
+        for a in range(K_PASSES):
+            quantize_w1(a, 0)
+            nc.vector.tensor_copy(v_codes[:, a, :], tab_w[a][:].bitcast(U32).indirect(lists[0][:]))
+            bent_pass(curved, a, 0)
+            direct_pass(direct, a, 0)
+            if a < 2:
+                nc.vector.tensor_copy(cand_planes[a][:], cand_sc[a][:].indirect(lists[1 + a][:]))
+        bent = tanh_out(curved, 0)
+        curved = [bank(PACK + t, "curved1%d" % t) for t in range(PACK)]
+        for a in range(K_PASSES):
+            bent_pass(curved, a, 1)
+        quantize_w1(0, 1)
+        make_h(direct, bent, 0)
+
+        direct = [bank(t, "direct1%d" % t) for t in range(PACK)]
+        direct_pass(direct, 0, 1)
+        quantize_w1(1, 1)
+        direct_pass(direct, 1, 1)
+        bent = tanh_out(curved, 1)
+        gather_cand(0, 0, 1)
+        e2 = [bank(PACK + i, "e2%d" % i) for i in range(M_TILES)]
+        for i in range(M_TILES):
+            score_pass(e2[i], 0, 0, i)
+        quantize_w1(2, 1)
+        direct_pass(direct, 2, 1)
+        gather_cand(0, 1, 1)
+        make_h(direct, bent, 1)
+        gather_cand(1, 0, 1)
+        e3 = [bank(i, "e3%d" % i) for i in range(M_TILES)]
+        for i in range(M_TILES):
+            score_pass(e2[i], 0, 1, i)
+        for i in range(M_TILES):
+            score_pass(e3[i], 1, 0, i)
+        for i in range(M_TILES):
+            nc.vector.tensor_tensor(out=cap_sb[:, i, :], in0=e2[i][:], in1=cap_sb[:, i, :], op=ALU.min)
+        gather_cand(1, 1, 2)
+        for i in range(M_TILES):
+            score_pass(e3[i], 1, 1, i)
+            nc.vector.tensor_tensor(out=cap_sb[:, i, :], in0=e3[i][:], in1=cap_sb[:, i, :], op=ALU.add)
+            nc.sync.dma_start(out=out[i * P : (i + 1) * P, :], in_=cap_sb[:, i, :])

@@ -24,6 +24,7 @@ R_PASSES = H // KP
 M_TILES = S // P
 LIST_COLS = S // 16
 CAND_ROW = (4, 8)
+SCALAR_SHARE = ((128, 128, 128), (0, 128, 64))
 
 
 def tile_list_graft_sharing_score_kernel(
@@ -34,7 +35,7 @@ def tile_list_graft_sharing_score_kernel(
     with ExitStack() as ctx:
         keep = ctx.enter_context(tc.tile_pool(name="keep", bufs=1))
         ring = ctx.enter_context(tc.tile_pool(name="ring", bufs=3))
-        stream = ctx.enter_context(tc.tile_pool(name="stream", bufs=5))
+        stream = ctx.enter_context(tc.tile_pool(name="stream", bufs=14))
         psum = ctx.enter_context(tc.psum_pool(name="psum", bufs=1))
 
         def held(name, shape, dtype):
@@ -50,11 +51,11 @@ def tile_list_graft_sharing_score_kernel(
 
         tab_sc = staged("tab_sc", [P, K_PASSES, T], U8)
         w4_sc_raw = staged("w4_sc_raw", [P, K_PASSES, H], U8)
-        cand_sc = [held("cand_sc%d" % n, [P, T], U8) for n in range(2)]
+        cand_sc = [staged("cand_sc%d" % n, [P, T], U8) for n in range(2)]
         nc.vector.memset(tab_sc[:].bitcast(I32), 0)
-        for n in range(2):
-            nc.gpsimd.memset(cand_sc[n][:].bitcast(I32), 0)
         nc.vector.memset(w4_sc_raw[:].bitcast(I32), 0)
+        for n in range(2):
+            nc.vector.memset(cand_sc[n][:].bitcast(I32), 0)
 
         def load_planes(dst, src):
             for q in range(4):
@@ -66,15 +67,13 @@ def tile_list_graft_sharing_score_kernel(
         def load_packed(n, src):
             for q in range(4):
                 first = 32 * q + CAND_ROW[n]
-                nc.gpsimd.dma_start(
+                nc.sync.dma_start(
                     out=cand_sc[n][first : first + 4 * R_PASSES, :].bitcast(I32),
                     in_=src[:, 4 * q : 4 * q + 4, :].bitcast(I32),
                 )
 
-        load_packed(0, tab2_scales)
-        load_packed(1, tab3_scales)
 
-        w4_raw = [staged("w4_raw%d" % a, [P, 2 * H], U8) for a in range(K_PASSES)]
+        w4_raw = {}
         w1_raw = {}
         tab_w = []
         cand_w = {}
@@ -91,23 +90,44 @@ def tile_list_graft_sharing_score_kernel(
             nc.sync.dma_start(out=words[:], in_=src.rearrange("p t i -> p (t i)").bitcast(I32))
             return words
 
-        for n, src in enumerate((offs, offs2, offs3)):
-            nc.sync.dma_start(lists[n][:], src)
+        nc.sync.dma_start(lists[0][:], offs)
+        def load_w4(b):
+            for a in range(K_PASSES):
+                w4_raw[a, b] = held("w4_raw%d%d" % (a, b), [P, 2 * KP], U8)
+                nc.sync.dma_start(
+                    out=w4_raw[a, b][:].bitcast(I32), in_=w4_words[a, :, 2 * b * KP : 2 * (b + 1) * KP].bitcast(I32)
+                )
+
+        def load_w4_rest():
+            rest = staged("w4_raw_rest", [P, K_PASSES, 2 * KP], U8)
+            nc.sync.dma_start(
+                out=rest[:].bitcast(I32), in_=w4_words[:, :, 2 * KP :].rearrange("a p c -> p a c").bitcast(I32)
+            )
+            for a in range(K_PASSES):
+                w4_raw[a, 1] = rest[:, a, :]
+
+        load_w4(0)
+        nc.sync.dma_start(lists[1][:], offs2)
+        nc.sync.dma_start(lists[2][:], offs3)
         bias = held("bias", [P, R_PASSES, PACK], F32)
         gains = held("gains", [P, R_PASSES, PACK], F32)
         nc.gpsimd.dma_start(out=bias[:], in_=b4.rearrange("(b p t) -> p b t", p=P, t=PACK))
         nc.gpsimd.dma_start(out=gains[:], in_=gain.rearrange("(b p t) -> p b t", p=P, t=PACK))
-        for a in range(K_PASSES):
-            nc.sync.dma_start(out=w4_raw[a][:].bitcast(I32), in_=w4_words[a].bitcast(I32))
         load_planes(tab_sc, tab_scales)
         load_planes(w4_sc_raw, w4_scales)
-        for a in range(K_PASSES):
-            load_w1(a, 0)
-            tab_w.append(load_words("tab_w%d" % a, tab_words[a]))
+        load_w1(0, 0)
+        tab_w.append(load_words("tab_w0", tab_words[0]))
+        load_packed(0, tab2_scales)
+        load_w1(1, 0)
+        tab_w.append(load_words("tab_w1", tab_words[1]))
+        load_packed(1, tab3_scales)
+        load_w1(2, 0)
+        load_w4_rest()
+        tab_w.append(load_words("tab_w2", tab_words[2]))
         load_w1(0, 1)
         load_w1(1, 1)
-        cand_w[0, 0] = load_words("cand_w00", tab2_words[0])
         load_w1(2, 1)
+        cand_w[0, 0] = load_words("cand_w00", tab2_words[0])
         cand_w[0, 1] = load_words("cand_w01", tab2_words[1])
         cand_w[1, 0] = load_words("cand_w10", tab3_words[0])
         cap_sb = staged("cap_sb", [P, M_TILES, S], F32)
@@ -116,10 +136,10 @@ def tile_list_graft_sharing_score_kernel(
 
         w4_codes = held("w4_codes", [P, K_PASSES, 2 * H], U8)
         w4_sc = held("w4_sc", [P, K_PASSES, H], U8)
-        for a in range(K_PASSES):
+        for (a, b), raw in w4_raw.items():
             nc.scalar.copy(
-                out=w4_codes[:, a, :].bitcast(U16).rearrange("p (b t m) -> p b t m", b=R_PASSES, t=PACK),
-                in_=w4_raw[a][:].bitcast(U16).rearrange("p (b m t) -> p b t m", b=R_PASSES, t=PACK),
+                out=w4_codes[:, a, 2 * b * KP : 2 * (b + 1) * KP].bitcast(U16).rearrange("p (t m) -> p t m", t=PACK),
+                in_=raw[:].bitcast(U16).rearrange("p (m t) -> p t m", t=PACK),
             )
 
         v_codes = held("v_codes", [P, K_PASSES, S], U32)
@@ -137,10 +157,17 @@ def tile_list_graft_sharing_score_kernel(
 
         def quantize_w1(a, b):
             grouped = ring.tile([P, PACK, P, PACK], BF16, name="w1_grouped", align_bytes=64)
-            nc.scalar.copy(
-                out=grouped[:].rearrange("p t m j -> p m j t"),
-                in_=w1_raw[a, b][:].rearrange("p j (m t) -> p m j t", t=PACK),
-            )
+            cut = SCALAR_SHARE[b][a]
+            if cut > 0:
+                nc.scalar.copy(
+                    out=grouped[:, :, :cut, :].rearrange("p t m j -> p m j t"),
+                    in_=w1_raw[a, b][:, :, : PACK * cut].rearrange("p j (m t) -> p m j t", t=PACK),
+                )
+            if cut < P:
+                nc.vector.tensor_copy(
+                    out=grouped[:, :, cut:, :].rearrange("p t m j -> p m j t"),
+                    in_=w1_raw[a, b][:, :, PACK * cut :].rearrange("p j (m t) -> p m j t", t=PACK),
+                )
             w1_codes[a, b] = held("w1_codes%d%d" % (a, b), [P, KP], U32)
             w1_sc[a, b] = held("w1_sc%d%d" % (a, b), [P, KP], U8)
             nc.vector.quantize_mx(
@@ -178,7 +205,7 @@ def tile_list_graft_sharing_score_kernel(
         def tanh_out(acc, b):
             bent = []
             for t in range(PACK):
-                bent.append(keep.tile([P, S], F32, name="bent%d%d" % (b, t), tag="bent%d" % t, align_bytes=64))
+                bent.append(keep.tile([P, S], F32, name="bent%d%d" % (b, t), align_bytes=64))
                 nc.scalar.activation(out=bent[t][:], in_=acc[t][:], func=ACT.Tanh, bias=bias[:, b, t : t + 1])
             return bent
 
@@ -189,9 +216,12 @@ def tile_list_graft_sharing_score_kernel(
             rows = keep.tile([P, PACK, S], BF16, name="h_rows%d" % b, tag="h_rows", align_bytes=64)
             for t in range(PACK):
                 nc.vector.tensor_tensor(out=bent[t][:], in0=direct[t][:], in1=bent[t][:], op=ALU.max)
-                nc.scalar.activation(out=rows[:, t, :], in_=bent[t][:], func=ACT.Copy, scale=gains[:, b, t : t + 1])
+                nc.gpsimd.tensor_scalar(
+                    out=rows[:, t, :], in0=bent[t][:], scalar1=gains[:, b, t : t + 1], scalar2=0.0,
+                    op0=ALU.mult, op1=ALU.add,
+                )
             grouped = keep.tile([P, S, PACK], BF16, name="h_grouped%d" % b, tag="h_grouped", align_bytes=64)
-            nc.vector.tensor_copy(
+            (nc.vector.tensor_copy, nc.vector.tensor_copy)[b](
                 out=grouped[:].rearrange("p (c i) t -> p c t i", i=4),
                 in_=rows[:].rearrange("p t (c i) -> p c t i", i=4),
             )
@@ -202,7 +232,11 @@ def tile_list_graft_sharing_score_kernel(
             )
 
         cand_codes = {}
-        cand_planes = [held("cand_planes%d" % n, [P, S], U8) for n in range(2)]
+        cand_planes = []
+
+        def gather_planes(n):
+            cand_planes.append(keep.tile([P, S], U8, name="cand_planes%d" % n, tag=("cp0", "cp1")[n], align_bytes=64))
+            nc.vector.tensor_copy(cand_planes[n][:], cand_sc[n][:].indirect(lists[1 + n][:]))
 
         def gather_cand(n, b, pieces):
             cand_codes[n, b] = held("cand_codes%d%d" % (n, b), [P, S], U32)
@@ -228,36 +262,32 @@ def tile_list_graft_sharing_score_kernel(
         direct = [bank(t, "direct0%d" % t) for t in range(PACK)]
         curved = [bank(PACK + t, "curved0%d" % t) for t in range(PACK)]
         for a in range(K_PASSES):
-            quantize_w1(a, 0)
             nc.vector.tensor_copy(v_codes[:, a, :], tab_w[a][:].bitcast(U32).indirect(lists[0][:]))
             bent_pass(curved, a, 0)
+            quantize_w1(a, 0)
             direct_pass(direct, a, 0)
-            if a < 2:
-                nc.vector.tensor_copy(cand_planes[a][:], cand_sc[a][:].indirect(lists[1 + a][:]))
         bent = tanh_out(curved, 0)
         curved = [bank(PACK + t, "curved1%d" % t) for t in range(PACK)]
         for a in range(K_PASSES):
             bent_pass(curved, a, 1)
-        quantize_w1(0, 1)
         make_h(direct, bent, 0)
 
         direct = [bank(t, "direct1%d" % t) for t in range(PACK)]
-        direct_pass(direct, 0, 1)
-        quantize_w1(1, 1)
-        direct_pass(direct, 1, 1)
-        bent = tanh_out(curved, 1)
-        gather_cand(0, 0, 1)
-        e2 = [bank(PACK + i, "e2%d" % i) for i in range(M_TILES)]
-        for i in range(M_TILES):
-            score_pass(e2[i], 0, 0, i)
-        quantize_w1(2, 1)
-        direct_pass(direct, 2, 1)
-        gather_cand(0, 1, 1)
+        for a in range(K_PASSES):
+            if a == 1:
+                bent = tanh_out(curved, 1)
+            quantize_w1(a, 1)
+            direct_pass(direct, a, 1)
         make_h(direct, bent, 1)
-        gather_cand(1, 0, 1)
+        gather_planes(0)
+        gather_planes(1)
+        e2 = [bank(PACK + i, "e2%d" % i) for i in range(M_TILES)]
         e3 = [bank(i, "e3%d" % i) for i in range(M_TILES)]
-        for i in range(M_TILES):
-            score_pass(e2[i], 0, 1, i)
+        for b in range(R_PASSES):
+            gather_cand(0, b, 1)
+            for i in range(M_TILES):
+                score_pass(e2[i], 0, b, i)
+        gather_cand(1, 0, 1)
         for i in range(M_TILES):
             score_pass(e3[i], 1, 0, i)
         for i in range(M_TILES):
@@ -265,5 +295,10 @@ def tile_list_graft_sharing_score_kernel(
         gather_cand(1, 1, 2)
         for i in range(M_TILES):
             score_pass(e3[i], 1, 1, i)
-            nc.vector.tensor_tensor(out=cap_sb[:, i, :], in0=e3[i][:], in1=cap_sb[:, i, :], op=ALU.add)
+            if i in (0, 2):
+                e3_sb = held("e3_sb%d" % i, [P, S], F32)
+                nc.scalar.copy(out=e3_sb[:], in_=e3[i][:])
+                nc.gpsimd.tensor_tensor(out=cap_sb[:, i, :], in0=e3_sb[:], in1=cap_sb[:, i, :], op=ALU.add)
+            else:
+                nc.vector.tensor_tensor(out=cap_sb[:, i, :], in0=e3[i][:], in1=cap_sb[:, i, :], op=ALU.add)
             nc.sync.dma_start(out=out[i * P : (i + 1) * P, :], in_=cap_sb[:, i, :])

@@ -18,13 +18,13 @@ ACT = mybir.ActivationFunctionType
 
 P = 128
 PACK = 4
-KP = P * PACK
-K_PASSES = K // KP
-R_PASSES = H // KP
+PASS = P * PACK
+K_PASSES = K // PASS
+R_PASSES = H // PASS
 M_TILES = S // P
-LIST_COLS = S // 16
+QUADRANTS = 4
 CAND_ROW = (4, 8)
-SCALAR_SHARE = ((128, 128, 128), (0, 128, 64))
+STAGED_BUFS = 13
 
 
 def tile_list_graft_sharing_score_kernel(
@@ -32,10 +32,12 @@ def tile_list_graft_sharing_score_kernel(
     w1, w4_words, w4_scales, b4, gain, cap, out,
 ):
     nc = tc.nc
+    cand_words = (tab2_words, tab3_words)
+    cand_scales = (tab2_scales, tab3_scales)
     with ExitStack() as ctx:
         keep = ctx.enter_context(tc.tile_pool(name="keep", bufs=1))
-        ring = ctx.enter_context(tc.tile_pool(name="ring", bufs=3))
-        stream = ctx.enter_context(tc.tile_pool(name="stream", bufs=14))
+        rounded = ctx.enter_context(tc.tile_pool(name="rounded", bufs=3))
+        stream = ctx.enter_context(tc.tile_pool(name="stream", bufs=STAGED_BUFS))
         psum = ctx.enter_context(tc.psum_pool(name="psum", bufs=1))
 
         def held(name, shape, dtype):
@@ -47,42 +49,21 @@ def tile_list_graft_sharing_score_kernel(
         def bank(n, name):
             return psum.tile([P, S], F32, name=name, tag="bank%d" % n)
 
-        lists = [held("list%d" % n, [P, LIST_COLS], U16) for n in range(3)]
-
         tab_sc = staged("tab_sc", [P, K_PASSES, T], U8)
         w4_sc_raw = staged("w4_sc_raw", [P, K_PASSES, H], U8)
         cand_sc = [staged("cand_sc%d" % n, [P, T], U8) for n in range(2)]
-        nc.vector.memset(tab_sc[:].bitcast(I32), 0)
-        nc.vector.memset(w4_sc_raw[:].bitcast(I32), 0)
-        for n in range(2):
-            nc.vector.memset(cand_sc[n][:].bitcast(I32), 0)
+        for zeroed in [tab_sc, w4_sc_raw] + cand_sc:
+            nc.vector.memset(zeroed[:].bitcast(I32), 0)
 
-        def load_planes(dst, src):
-            for q in range(4):
-                nc.sync.dma_start(
-                    out=dst[32 * q : 32 * q + 4, :, :].bitcast(I32),
-                    in_=src[:, 4 * q : 4 * q + 4, :].rearrange("a r t -> r a t").bitcast(I32),
-                )
-
-        def load_packed(n, src):
-            for q in range(4):
-                first = 32 * q + CAND_ROW[n]
-                nc.sync.dma_start(
-                    out=cand_sc[n][first : first + 4 * R_PASSES, :].bitcast(I32),
-                    in_=src[:, 4 * q : 4 * q + 4, :].bitcast(I32),
-                )
-
-
-        w4_raw = {}
+        lists = [held("list%d" % n, [P, S // 16], U16) for n in range(3)]
+        w4_raw = [held("w4_raw%d" % a, [P, 2 * H], U8) for a in range(K_PASSES)]
         w1_raw = {}
-        tab_w = []
-        cand_w = {}
 
-        def load_w1(a, b):
-            w1_raw[a, b] = staged("w1_raw%d%d" % (a, b), [P, PACK, KP], F32)
+        def load_w1(a, b, place):
+            w1_raw[a, b] = place("w1_raw%d%d" % (a, b), [P, PACK, PASS], F32)
             nc.sync.dma_start(
                 out=w1_raw[a, b][:],
-                in_=w1[a * KP : (a + 1) * KP, b * KP : (b + 1) * KP].rearrange("(p j) c -> p j c", j=PACK),
+                in_=w1[a * PASS : (a + 1) * PASS, b * PASS : (b + 1) * PASS].rearrange("(p j) c -> p j c", j=PACK),
             )
 
         def load_words(name, src):
@@ -91,57 +72,51 @@ def tile_list_graft_sharing_score_kernel(
             return words
 
         nc.sync.dma_start(lists[0][:], offs)
-        def load_w4(b):
-            for a in range(K_PASSES):
-                w4_raw[a, b] = held("w4_raw%d%d" % (a, b), [P, 2 * KP], U8)
-                nc.sync.dma_start(
-                    out=w4_raw[a, b][:].bitcast(I32), in_=w4_words[a, :, 2 * b * KP : 2 * (b + 1) * KP].bitcast(I32)
-                )
-
-        def load_w4_rest():
-            rest = staged("w4_raw_rest", [P, K_PASSES, 2 * KP], U8)
-            nc.sync.dma_start(
-                out=rest[:].bitcast(I32), in_=w4_words[:, :, 2 * KP :].rearrange("a p c -> p a c").bitcast(I32)
-            )
-            for a in range(K_PASSES):
-                w4_raw[a, 1] = rest[:, a, :]
-
-        load_w4(0)
+        for a in range(K_PASSES):
+            nc.sync.dma_start(out=w4_raw[a][:].bitcast(I32), in_=w4_words[a].bitcast(I32))
+        load_w1(0, 0, held)
         nc.sync.dma_start(lists[1][:], offs2)
         nc.sync.dma_start(lists[2][:], offs3)
         bias = held("bias", [P, R_PASSES, PACK], F32)
         gains = held("gains", [P, R_PASSES, PACK], F32)
         nc.gpsimd.dma_start(out=bias[:], in_=b4.rearrange("(b p t) -> p b t", p=P, t=PACK))
         nc.gpsimd.dma_start(out=gains[:], in_=gain.rearrange("(b p t) -> p b t", p=P, t=PACK))
-        load_planes(tab_sc, tab_scales)
-        load_planes(w4_sc_raw, w4_scales)
-        load_w1(0, 0)
-        tab_w.append(load_words("tab_w0", tab_words[0]))
-        load_packed(0, tab2_scales)
-        load_w1(1, 0)
-        tab_w.append(load_words("tab_w1", tab_words[1]))
-        load_packed(1, tab3_scales)
-        load_w1(2, 0)
-        load_w4_rest()
-        tab_w.append(load_words("tab_w2", tab_words[2]))
-        load_w1(0, 1)
-        load_w1(1, 1)
-        load_w1(2, 1)
-        cand_w[0, 0] = load_words("cand_w00", tab2_words[0])
-        cand_w[0, 1] = load_words("cand_w01", tab2_words[1])
-        cand_w[1, 0] = load_words("cand_w10", tab3_words[0])
-        cap_sb = staged("cap_sb", [P, M_TILES, S], F32)
-        nc.sync.dma_start(out=cap_sb[:], in_=cap.rearrange("(i p) j -> p i j", p=P))
-        cand_w[1, 1] = load_words("cand_w11", tab3_words[1])
+
+        for dst, src in ((tab_sc, tab_scales), (w4_sc_raw, w4_scales)):
+            for q in range(QUADRANTS):
+                nc.sync.dma_start(
+                    out=dst[32 * q : 32 * q + 4, :, :].bitcast(I32),
+                    in_=src[:, 4 * q : 4 * q + 4, :].rearrange("a s t -> s a t").bitcast(I32),
+                )
+        for n in range(2):
+            for q in range(QUADRANTS):
+                first = 32 * q + CAND_ROW[n]
+                nc.sync.dma_start(
+                    out=cand_sc[n][first : first + 4 * R_PASSES, :].bitcast(I32),
+                    in_=cand_scales[n][:, 4 * q : 4 * q + 4, :].bitcast(I32),
+                )
+
+        tab_w = []
+        for a in range(K_PASSES):
+            if a > 0:
+                load_w1(a, 0, staged)
+            tab_w.append(load_words("tab_w%d" % a, tab_words[a]))
+        for a in range(K_PASSES):
+            load_w1(a, 1, staged)
+        cand_w = {}
+        for n, b in ((0, 0), (0, 1), (1, 0)):
+            cand_w[n, b] = load_words("cand_w%d%d" % (n, b), cand_words[n][b])
+        result = staged("result", [P, M_TILES, S], F32)
+        nc.sync.dma_start(out=result[:], in_=cap.rearrange("(i p) j -> p i j", p=P))
+        cand_w[1, 1] = load_words("cand_w11", cand_words[1][1])
 
         w4_codes = held("w4_codes", [P, K_PASSES, 2 * H], U8)
         w4_sc = held("w4_sc", [P, K_PASSES, H], U8)
-        for (a, b), raw in w4_raw.items():
+        for a in range(K_PASSES):
             nc.scalar.copy(
-                out=w4_codes[:, a, 2 * b * KP : 2 * (b + 1) * KP].bitcast(U16).rearrange("p (t m) -> p t m", t=PACK),
-                in_=raw[:].bitcast(U16).rearrange("p (m t) -> p t m", t=PACK),
+                out=w4_codes[:, a, :].bitcast(U16).rearrange("p (b t m) -> p b t m", b=R_PASSES, t=PACK),
+                in_=w4_raw[a][:].bitcast(U16).rearrange("p (b m t) -> p b t m", b=R_PASSES, t=PACK),
             )
-
         v_codes = held("v_codes", [P, K_PASSES, S], U32)
         v_sc = held("v_sc", [P, K_PASSES, S], U8)
         for a in range(K_PASSES):
@@ -156,29 +131,27 @@ def tile_list_graft_sharing_score_kernel(
         w1_sc = {}
 
         def quantize_w1(a, b):
-            grouped = ring.tile([P, PACK, P, PACK], BF16, name="w1_grouped", align_bytes=64)
-            cut = SCALAR_SHARE[b][a]
-            if cut > 0:
-                nc.scalar.copy(
-                    out=grouped[:, :, :cut, :].rearrange("p t m j -> p m j t"),
-                    in_=w1_raw[a, b][:, :, : PACK * cut].rearrange("p j (m t) -> p m j t", t=PACK),
-                )
-            if cut < P:
+            grouped = rounded.tile([P, PACK, P, PACK], BF16, name="w1_grouped", align_bytes=64)
+            if (a, b) == (0, 1):
                 nc.vector.tensor_copy(
-                    out=grouped[:, :, cut:, :].rearrange("p t m j -> p m j t"),
-                    in_=w1_raw[a, b][:, :, PACK * cut :].rearrange("p j (m t) -> p m j t", t=PACK),
+                    out=grouped[:], in_=w1_raw[a, b][:].rearrange("p j (m t) -> p t m j", t=PACK)
                 )
-            w1_codes[a, b] = held("w1_codes%d%d" % (a, b), [P, KP], U32)
-            w1_sc[a, b] = held("w1_sc%d%d" % (a, b), [P, KP], U8)
+            else:
+                nc.scalar.copy(
+                    out=grouped[:].rearrange("p t m j -> p m t j"),
+                    in_=w1_raw[a, b][:].rearrange("p j (m t) -> p m t j", t=PACK),
+                )
+            w1_codes[a, b] = held("w1_codes%d%d" % (a, b), [P, PASS], U32)
+            w1_sc[a, b] = held("w1_sc%d%d" % (a, b), [P, PASS], U8)
             nc.vector.quantize_mx(
                 out=w1_codes[a, b][:].bitcast(FP8X4),
                 scales=w1_sc[a, b][:],
                 in_=grouped[:].rearrange("p t m j -> p (t m j)"),
             )
 
-        def bent_pass(acc, a, b):
+        def curved_pass(acc, a, b):
             for t in range(PACK):
-                c0 = b * KP + t * P
+                c0 = b * PASS + t * P
                 nc.tensor.matmul_mx(
                     out=acc[t][:],
                     lhsT=w4_codes[:, a, 2 * c0 : 2 * (c0 + P)].bitcast(FP4X4),
@@ -203,9 +176,8 @@ def tile_list_graft_sharing_score_kernel(
                 )
 
         def tanh_out(acc, b):
-            bent = []
+            bent = [held("bent%d%d" % (b, t), [P, S], F32) for t in range(PACK)]
             for t in range(PACK):
-                bent.append(keep.tile([P, S], F32, name="bent%d%d" % (b, t), align_bytes=64))
                 nc.scalar.activation(out=bent[t][:], in_=acc[t][:], func=ACT.Tanh, bias=bias[:, b, t : t + 1])
             return bent
 
@@ -216,12 +188,16 @@ def tile_list_graft_sharing_score_kernel(
             rows = keep.tile([P, PACK, S], BF16, name="h_rows%d" % b, tag="h_rows", align_bytes=64)
             for t in range(PACK):
                 nc.vector.tensor_tensor(out=bent[t][:], in0=direct[t][:], in1=bent[t][:], op=ALU.max)
-                nc.gpsimd.tensor_scalar(
-                    out=rows[:, t, :], in0=bent[t][:], scalar1=gains[:, b, t : t + 1], scalar2=0.0,
-                    op0=ALU.mult, op1=ALU.add,
-                )
+                if b == 0:
+                    nc.vector.tensor_scalar(
+                        out=rows[:, t, :], in0=bent[t][:], scalar1=gains[:, b, t : t + 1], scalar2=None, op0=ALU.mult
+                    )
+                else:
+                    nc.scalar.activation(
+                        out=rows[:, t, :], in_=bent[t][:], func=ACT.Copy, scale=gains[:, b, t : t + 1]
+                    )
             grouped = keep.tile([P, S, PACK], BF16, name="h_grouped%d" % b, tag="h_grouped", align_bytes=64)
-            (nc.vector.tensor_copy, nc.vector.tensor_copy)[b](
+            nc.vector.tensor_copy(
                 out=grouped[:].rearrange("p (c i) t -> p c t i", i=4),
                 in_=rows[:].rearrange("p t (c i) -> p c t i", i=4),
             )
@@ -231,12 +207,31 @@ def tile_list_graft_sharing_score_kernel(
                 out=h_codes[b][:].bitcast(FP8X4), scales=h_sc[b][:], in_=grouped[:].rearrange("p j t -> p (j t)")
             )
 
-        cand_codes = {}
-        cand_planes = []
+        direct = [bank(t, "direct0%d" % t) for t in range(PACK)]
+        curved = [bank(PACK + t, "curved0%d" % t) for t in range(PACK)]
+        for a in range(K_PASSES):
+            nc.vector.tensor_copy(v_codes[:, a, :], tab_w[a][:].bitcast(U32).indirect(lists[0][:]))
+            curved_pass(curved, a, 0)
+            quantize_w1(a, 0)
+            direct_pass(direct, a, 0)
+        bent = tanh_out(curved, 0)
+        curved = [bank(PACK + t, "curved1%d" % t) for t in range(PACK)]
+        for a in range(K_PASSES):
+            curved_pass(curved, a, 1)
+        make_h(direct, bent, 0)
 
-        def gather_planes(n):
-            cand_planes.append(keep.tile([P, S], U8, name="cand_planes%d" % n, tag=("cp0", "cp1")[n], align_bytes=64))
+        direct = [bank(t, "direct1%d" % t) for t in range(PACK)]
+        for a in range(K_PASSES):
+            if a == 1:
+                bent = tanh_out(curved, 1)
+            quantize_w1(a, 1)
+            direct_pass(direct, a, 1)
+        make_h(direct, bent, 1)
+
+        cand_planes = [held("cand_planes%d" % n, [P, S], U8) for n in range(2)]
+        for n in range(2):
             nc.vector.tensor_copy(cand_planes[n][:], cand_sc[n][:].indirect(lists[1 + n][:]))
+        cand_codes = {}
 
         def gather_cand(n, b, pieces):
             cand_codes[n, b] = held("cand_codes%d%d" % (n, b), [P, S], U32)
@@ -259,28 +254,6 @@ def tile_list_graft_sharing_score_kernel(
                 stop=(b == R_PASSES - 1),
             )
 
-        direct = [bank(t, "direct0%d" % t) for t in range(PACK)]
-        curved = [bank(PACK + t, "curved0%d" % t) for t in range(PACK)]
-        for a in range(K_PASSES):
-            nc.vector.tensor_copy(v_codes[:, a, :], tab_w[a][:].bitcast(U32).indirect(lists[0][:]))
-            bent_pass(curved, a, 0)
-            quantize_w1(a, 0)
-            direct_pass(direct, a, 0)
-        bent = tanh_out(curved, 0)
-        curved = [bank(PACK + t, "curved1%d" % t) for t in range(PACK)]
-        for a in range(K_PASSES):
-            bent_pass(curved, a, 1)
-        make_h(direct, bent, 0)
-
-        direct = [bank(t, "direct1%d" % t) for t in range(PACK)]
-        for a in range(K_PASSES):
-            if a == 1:
-                bent = tanh_out(curved, 1)
-            quantize_w1(a, 1)
-            direct_pass(direct, a, 1)
-        make_h(direct, bent, 1)
-        gather_planes(0)
-        gather_planes(1)
         e2 = [bank(PACK + i, "e2%d" % i) for i in range(M_TILES)]
         e3 = [bank(i, "e3%d" % i) for i in range(M_TILES)]
         for b in range(R_PASSES):
@@ -291,14 +264,9 @@ def tile_list_graft_sharing_score_kernel(
         for i in range(M_TILES):
             score_pass(e3[i], 1, 0, i)
         for i in range(M_TILES):
-            nc.vector.tensor_tensor(out=cap_sb[:, i, :], in0=e2[i][:], in1=cap_sb[:, i, :], op=ALU.min)
+            nc.vector.tensor_tensor(out=result[:, i, :], in0=e2[i][:], in1=result[:, i, :], op=ALU.min)
         gather_cand(1, 1, 2)
         for i in range(M_TILES):
             score_pass(e3[i], 1, 1, i)
-            if i in (0, 2):
-                e3_sb = held("e3_sb%d" % i, [P, S], F32)
-                nc.scalar.copy(out=e3_sb[:], in_=e3[i][:])
-                nc.gpsimd.tensor_tensor(out=cap_sb[:, i, :], in0=e3_sb[:], in1=cap_sb[:, i, :], op=ALU.add)
-            else:
-                nc.vector.tensor_tensor(out=cap_sb[:, i, :], in0=e3[i][:], in1=cap_sb[:, i, :], op=ALU.add)
-            nc.sync.dma_start(out=out[i * P : (i + 1) * P, :], in_=cap_sb[:, i, :])
+            nc.vector.tensor_tensor(out=result[:, i, :], in0=e3[i][:], in1=result[:, i, :], op=ALU.add)
+            nc.sync.dma_start(out=out[i * P : (i + 1) * P, :], in_=result[:, i, :])

@@ -59,8 +59,8 @@ def tile_list_graft_sharing_score_kernel(
         w4_raw = [held("w4_raw%d" % a, [P, 2 * H], U8) for a in range(K_PASSES)]
         w1_raw = {}
 
-        def load_w1(a, b, place):
-            w1_raw[a, b] = place("w1_raw%d%d" % (a, b), [P, PACK, PASS], F32)
+        def load_w1(a, b):
+            w1_raw[a, b] = staged("w1_raw%d%d" % (a, b), [P, PACK, PASS], F32)
             nc.sync.dma_start(
                 out=w1_raw[a, b][:],
                 in_=w1[a * PASS : (a + 1) * PASS, b * PASS : (b + 1) * PASS].rearrange("(p j) c -> p j c", j=PACK),
@@ -74,7 +74,6 @@ def tile_list_graft_sharing_score_kernel(
         nc.sync.dma_start(lists[0][:], offs)
         for a in range(K_PASSES):
             nc.sync.dma_start(out=w4_raw[a][:].bitcast(I32), in_=w4_words[a].bitcast(I32))
-        load_w1(0, 0, held)
         nc.sync.dma_start(lists[1][:], offs2)
         nc.sync.dma_start(lists[2][:], offs3)
         bias = held("bias", [P, R_PASSES, PACK], F32)
@@ -98,17 +97,16 @@ def tile_list_graft_sharing_score_kernel(
 
         tab_w = []
         for a in range(K_PASSES):
-            if a > 0:
-                load_w1(a, 0, staged)
+            load_w1(a, 0)
             tab_w.append(load_words("tab_w%d" % a, tab_words[a]))
         for a in range(K_PASSES):
-            load_w1(a, 1, staged)
+            load_w1(a, 1)
         cand_w = {}
-        for n, b in ((0, 0), (0, 1), (1, 0)):
-            cand_w[n, b] = load_words("cand_w%d%d" % (n, b), cand_words[n][b])
+        for b in range(R_PASSES):
+            for n in range(2):
+                cand_w[n, b] = load_words("cand_w%d%d" % (n, b), cand_words[n][b])
         result = staged("result", [P, M_TILES, S], F32)
         nc.sync.dma_start(out=result[:], in_=cap.rearrange("(i p) j -> p i j", p=P))
-        cand_w[1, 1] = load_words("cand_w11", cand_words[1][1])
 
         w4_codes = held("w4_codes", [P, K_PASSES, 2 * H], U8)
         w4_sc = held("w4_sc", [P, K_PASSES, H], U8)
@@ -132,15 +130,11 @@ def tile_list_graft_sharing_score_kernel(
 
         def quantize_w1(a, b):
             grouped = rounded.tile([P, PACK, P, PACK], BF16, name="w1_grouped", align_bytes=64)
-            if (a, b) == (0, 1):
-                nc.vector.tensor_copy(
-                    out=grouped[:], in_=w1_raw[a, b][:].rearrange("p j (m t) -> p t m j", t=PACK)
-                )
-            else:
-                nc.scalar.copy(
-                    out=grouped[:].rearrange("p t m j -> p m t j"),
-                    in_=w1_raw[a, b][:].rearrange("p j (m t) -> p m t j", t=PACK),
-                )
+            copy = nc.vector.tensor_copy if (a, b) == (0, 1) else nc.scalar.copy
+            copy(
+                out=grouped[:].rearrange("p t m j -> p m t j"),
+                in_=w1_raw[a, b][:].rearrange("p j (m t) -> p m t j", t=PACK),
+            )
             w1_codes[a, b] = held("w1_codes%d%d" % (a, b), [P, PASS], U32)
             w1_sc[a, b] = held("w1_sc%d%d" % (a, b), [P, PASS], U8)
             nc.vector.quantize_mx(
@@ -184,8 +178,8 @@ def tile_list_graft_sharing_score_kernel(
         h_codes = []
         h_sc = []
 
-        def make_h(direct, bent, b):
-            rows = keep.tile([P, PACK, S], BF16, name="h_rows%d" % b, tag="h_rows", align_bytes=64)
+        def h_rows(direct, bent, b):
+            rows = held("h_rows%d" % b, [P, PACK, S], BF16)
             for t in range(PACK):
                 nc.vector.tensor_tensor(out=bent[t][:], in0=direct[t][:], in1=bent[t][:], op=ALU.max)
                 if b == 0:
@@ -196,8 +190,11 @@ def tile_list_graft_sharing_score_kernel(
                     nc.scalar.activation(
                         out=rows[:, t, :], in_=bent[t][:], func=ACT.Copy, scale=gains[:, b, t : t + 1]
                     )
-            grouped = keep.tile([P, S, PACK], BF16, name="h_grouped%d" % b, tag="h_grouped", align_bytes=64)
-            nc.vector.tensor_copy(
+            return rows
+
+        def quantize_h(rows, b, copy):
+            grouped = held("h_grouped%d" % b, [P, S, PACK], BF16)
+            copy(
                 out=grouped[:].rearrange("p (c i) t -> p c t i", i=4),
                 in_=rows[:].rearrange("p t (c i) -> p c t i", i=4),
             )
@@ -218,29 +215,23 @@ def tile_list_graft_sharing_score_kernel(
         curved = [bank(PACK + t, "curved1%d" % t) for t in range(PACK)]
         for a in range(K_PASSES):
             curved_pass(curved, a, 1)
-        make_h(direct, bent, 0)
+        quantize_h(h_rows(direct, bent, 0), 0, nc.vector.tensor_copy)
 
         direct = [bank(t, "direct1%d" % t) for t in range(PACK)]
         for a in range(K_PASSES):
-            if a == 1:
-                bent = tanh_out(curved, 1)
             quantize_w1(a, 1)
             direct_pass(direct, a, 1)
-        make_h(direct, bent, 1)
+        bent = tanh_out(curved, 1)
+        quantize_h(h_rows(direct, bent, 1), 1, nc.scalar.copy)
 
         cand_planes = [held("cand_planes%d" % n, [P, S], U8) for n in range(2)]
         for n in range(2):
             nc.vector.tensor_copy(cand_planes[n][:], cand_sc[n][:].indirect(lists[1 + n][:]))
         cand_codes = {}
 
-        def gather_cand(n, b, pieces):
+        def gather_cand(n, b):
             cand_codes[n, b] = held("cand_codes%d%d" % (n, b), [P, S], U32)
-            width = S // pieces
-            for u in range(pieces):
-                nc.vector.tensor_copy(
-                    cand_codes[n, b][:, u * width : (u + 1) * width],
-                    cand_w[n, b][:].bitcast(U32).indirect(lists[1 + n][:, u * width // 16 : (u + 1) * width // 16]),
-                )
+            nc.vector.tensor_copy(cand_codes[n, b][:], cand_w[n, b][:].bitcast(U32).indirect(lists[1 + n][:]))
 
         def score_pass(acc, n, b, i):
             cols = slice(i * P, (i + 1) * P)
@@ -257,16 +248,11 @@ def tile_list_graft_sharing_score_kernel(
         e2 = [bank(PACK + i, "e2%d" % i) for i in range(M_TILES)]
         e3 = [bank(i, "e3%d" % i) for i in range(M_TILES)]
         for b in range(R_PASSES):
-            gather_cand(0, b, 1)
-            for i in range(M_TILES):
-                score_pass(e2[i], 0, b, i)
-        gather_cand(1, 0, 1)
-        for i in range(M_TILES):
-            score_pass(e3[i], 1, 0, i)
+            for n, acc in enumerate((e2, e3)):
+                gather_cand(n, b)
+                for i in range(M_TILES):
+                    score_pass(acc[i], n, b, i)
         for i in range(M_TILES):
             nc.vector.tensor_tensor(out=result[:, i, :], in0=e2[i][:], in1=result[:, i, :], op=ALU.min)
-        gather_cand(1, 1, 2)
-        for i in range(M_TILES):
-            score_pass(e3[i], 1, 1, i)
             nc.vector.tensor_tensor(out=result[:, i, :], in0=e3[i][:], in1=result[:, i, :], op=ALU.add)
             nc.sync.dma_start(out=out[i * P : (i + 1) * P, :], in_=result[:, i, :])

from contextlib import ExitStack

import concourse.mybir as mybir

K, H, T, S = 1536, 1024, 2048, 512
FLOPS = 2 * (2 * K * H * S + 2 * H * S * S)

F32 = mybir.dt.float32
BF16 = mybir.dt.bfloat16
I32 = mybir.dt.int32
U32 = mybir.dt.uint32
U16 = mybir.dt.uint16
U8 = mybir.dt.uint8
FP8X4 = mybir.dt.float8_e4m3fn_x4
FP4X4 = mybir.dt.float4_e2m1fn_x4
ALU = mybir.AluOpType
ACT = mybir.ActivationFunctionType

P = 128
PACK = 4
PASS = P * PACK
K_PASSES = K // PASS
R_PASSES = H // PASS
M_TILES = S // P
QUADRANTS = 4
CAND_ROW = (4, 8)
STAGED_BUFS = 13


def tile_list_graft_sharing_score_kernel(
    tc, tab_words, tab_scales, offs, tab2_words, tab2_scales, offs2, tab3_words, tab3_scales, offs3,
    w1, w4_words, w4_scales, b4, gain, cap, out,
):
    nc = tc.nc
    cand_words = (tab2_words, tab3_words)
    cand_scales = (tab2_scales, tab3_scales)
    with ExitStack() as ctx:
        keep = ctx.enter_context(tc.tile_pool(name="keep", bufs=1))
        rounded = ctx.enter_context(tc.tile_pool(name="rounded", bufs=3))
        stream = ctx.enter_context(tc.tile_pool(name="stream", bufs=STAGED_BUFS))
        psum = ctx.enter_context(tc.psum_pool(name="psum", bufs=1))

        def held(name, shape, dtype):
            return keep.tile(shape, dtype, name=name, align_bytes=64)

        def staged(name, shape, dtype):
            return stream.tile(shape, dtype, name=name, tag="staged", align_bytes=64)

        def bank(n, name):
            return psum.tile([P, S], F32, name=name, tag="bank%d" % n)

        tab_sc = staged("tab_sc", [P, K_PASSES, T], U8)
        w4_sc_raw = staged("w4_sc_raw", [P, K_PASSES, H], U8)
        cand_sc = [staged("cand_sc%d" % n, [P, T], U8) for n in range(2)]
        for zeroed in [tab_sc, w4_sc_raw] + cand_sc:
            nc.vector.memset(zeroed[:].bitcast(I32), 0)

        lists = [held("list%d" % n, [P, S // 16], U16) for n in range(3)]
        w4_raw = [held("w4_raw%d" % a, [P, 2 * H], U8) for a in range(K_PASSES)]
        w1_raw = {}

        def load_w1(a, b):
            w1_raw[a, b] = staged("w1_raw%d%d" % (a, b), [P, PACK, PASS], F32)
            nc.sync.dma_start(
                out=w1_raw[a, b][:],
                in_=w1[a * PASS : (a + 1) * PASS, b * PASS : (b + 1) * PASS].rearrange("(p j) c -> p j c", j=PACK),
            )

        def load_words(name, src):
            words = staged(name, [P, T], I32)
            nc.sync.dma_start(out=words[:], in_=src.rearrange("p t i -> p (t i)").bitcast(I32))
            return words

        nc.sync.dma_start(lists[0][:], offs)
        for a in range(K_PASSES):
            nc.sync.dma_start(out=w4_raw[a][:].bitcast(I32), in_=w4_words[a].bitcast(I32))
        nc.sync.dma_start(lists[1][:], offs2)
        nc.sync.dma_start(lists[2][:], offs3)
        bias = held("bias", [P, R_PASSES, PACK], F32)
        gains = held("gains", [P, R_PASSES, PACK], F32)
        nc.gpsimd.dma_start(out=bias[:], in_=b4.rearrange("(b p t) -> p b t", p=P, t=PACK))
        nc.gpsimd.dma_start(out=gains[:], in_=gain.rearrange("(b p t) -> p b t", p=P, t=PACK))

        for dst, src in ((tab_sc, tab_scales), (w4_sc_raw, w4_scales)):
            for q in range(QUADRANTS):
                nc.sync.dma_start(
                    out=dst[32 * q : 32 * q + 4, :, :].bitcast(I32),
                    in_=src[:, 4 * q : 4 * q + 4, :].rearrange("a s t -> s a t").bitcast(I32),
                )
        for n in range(2):
            for q in range(QUADRANTS):
                first = 32 * q + CAND_ROW[n]
                nc.sync.dma_start(
                    out=cand_sc[n][first : first + 4 * R_PASSES, :].bitcast(I32),
                    in_=cand_scales[n][:, 4 * q : 4 * q + 4, :].bitcast(I32),
                )

        tab_w = []
        for a in range(K_PASSES):
            load_w1(a, 0)
            tab_w.append(load_words("tab_w%d" % a, tab_words[a]))
        for a in range(K_PASSES):
            load_w1(a, 1)
        cand_w = {}
        for b in range(R_PASSES):
            for n in range(2):
                cand_w[n, b] = load_words("cand_w%d%d" % (n, b), cand_words[n][b])
        result = staged("result", [P, M_TILES, S], F32)
        nc.sync.dma_start(out=result[:], in_=cap.rearrange("(i p) j -> p i j", p=P))

        w4_codes = held("w4_codes", [P, K_PASSES, 2 * H], U8)
        w4_sc = held("w4_sc", [P, K_PASSES, H], U8)
        for a in range(K_PASSES):
            nc.scalar.copy(
                out=w4_codes[:, a, :].bitcast(U16).rearrange("p (b t m) -> p b t m", b=R_PASSES, t=PACK),
                in_=w4_raw[a][:].bitcast(U16).rearrange("p (b m t) -> p b t m", b=R_PASSES, t=PACK),
            )
        v_codes = held("v_codes", [P, K_PASSES, S], U32)
        v_sc = held("v_sc", [P, K_PASSES, S], U8)
        for a in range(K_PASSES):
            nc.vector.tensor_copy(v_sc[:, a, :], tab_sc[:, a, :].indirect(lists[0][:]))
        for a in range(K_PASSES):
            nc.vector.tensor_copy(
                out=w4_sc[:, a, :].rearrange("p (b t m) -> p b t m", b=R_PASSES, t=PACK),
                in_=w4_sc_raw[:, a, :].rearrange("p (b m t) -> p b t m", b=R_PASSES, t=PACK),
            )

        w1_codes = {}
        w1_sc = {}

        def quantize_w1(a, b):
            grouped = rounded.tile([P, PACK, P, PACK], BF16, name="w1_grouped", align_bytes=64)
            copy = nc.vector.tensor_copy if (a, b) == (0, 1) else nc.scalar.copy
            copy(
                out=grouped[:].rearrange("p t m j -> p m t j"),
                in_=w1_raw[a, b][:].rearrange("p j (m t) -> p m t j", t=PACK),
            )
            w1_codes[a, b] = held("w1_codes%d%d" % (a, b), [P, PASS], U32)
            w1_sc[a, b] = held("w1_sc%d%d" % (a, b), [P, PASS], U8)
            nc.vector.quantize_mx(
                out=w1_codes[a, b][:].bitcast(FP8X4),
                scales=w1_sc[a, b][:],
                in_=grouped[:].rearrange("p t m j -> p (t m j)"),
            )

        def curved_pass(acc, a, b):
            for t in range(PACK):
                c0 = b * PASS + t * P
                nc.tensor.matmul_mx(
                    out=acc[t][:],
                    lhsT=w4_codes[:, a, 2 * c0 : 2 * (c0 + P)].bitcast(FP4X4),
                    lhsT_scale=w4_sc[:, a, c0 : c0 + P],
                    rhs=v_codes[:, a, :].bitcast(FP8X4),
                    rhs_scale=v_sc[:, a, :],
                    start=(a == 0),
                    stop=(a == K_PASSES - 1),
                )

        def direct_pass(acc, a, b):
            for t in range(PACK):
                cols = slice(t * P, (t + 1) * P)
                nc.tensor.matmul_mx(
                    out=acc[t][:],
                    lhsT=w1_codes[a, b][:, cols].bitcast(FP8X4),
                    lhsT_scale=w1_sc[a, b][:, cols],
                    rhs=v_codes[:, a, :].bitcast(FP8X4),
                    rhs_scale=v_sc[:, a, :],
                    start=(a == 0),
                    stop=(a == K_PASSES - 1),
                )

        def tanh_out(acc, b):
            bent = [held("bent%d%d" % (b, t), [P, S], F32) for t in range(PACK)]
            for t in range(PACK):
                nc.scalar.activation(out=bent[t][:], in_=acc[t][:], func=ACT.Tanh, bias=bias[:, b, t : t + 1])
            return bent

        h_codes = []
        h_sc = []

        def h_rows(direct, bent, b):
            rows = held("h_rows%d" % b, [P, PACK, S], BF16)
            for t in range(PACK):
                nc.vector.tensor_tensor(out=bent[t][:], in0=direct[t][:], in1=bent[t][:], op=ALU.max)
                if b == 0:
                    nc.vector.tensor_scalar(
                        out=rows[:, t, :], in0=bent[t][:], scalar1=gains[:, b, t : t + 1], scalar2=None, op0=ALU.mult
                    )
                else:
                    nc.scalar.activation(
                        out=rows[:, t, :], in_=bent[t][:], func=ACT.Copy, scale=gains[:, b, t : t + 1]
                    )
            return rows

        def quantize_h(rows, b, copy):
            grouped = held("h_grouped%d" % b, [P, S, PACK], BF16)
            copy(
                out=grouped[:].rearrange("p (c i) t -> p c t i", i=4),
                in_=rows[:].rearrange("p t (c i) -> p c t i", i=4),
            )
            h_codes.append(held("h_codes%d" % b, [P, S], U32))
            h_sc.append(held("h_sc%d" % b, [P, S], U8))
            nc.vector.quantize_mx(
                out=h_codes[b][:].bitcast(FP8X4), scales=h_sc[b][:], in_=grouped[:].rearrange("p j t -> p (j t)")
            )

        direct = [bank(t, "direct0%d" % t) for t in range(PACK)]
        curved = [bank(PACK + t, "curved0%d" % t) for t in range(PACK)]
        for a in range(K_PASSES):
            nc.vector.tensor_copy(v_codes[:, a, :], tab_w[a][:].bitcast(U32).indirect(lists[0][:]))
            curved_pass(curved, a, 0)
            quantize_w1(a, 0)
            direct_pass(direct, a, 0)
        bent = tanh_out(curved, 0)
        curved = [bank(PACK + t, "curved1%d" % t) for t in range(PACK)]
        for a in range(K_PASSES):
            curved_pass(curved, a, 1)
        quantize_h(h_rows(direct, bent, 0), 0, nc.vector.tensor_copy)

        direct = [bank(t, "direct1%d" % t) for t in range(PACK)]
        for a in range(K_PASSES):
            quantize_w1(a, 1)
            direct_pass(direct, a, 1)
        bent = tanh_out(curved, 1)
        quantize_h(h_rows(direct, bent, 1), 1, nc.scalar.copy)

        cand_planes = [held("cand_planes%d" % n, [P, S], U8) for n in range(2)]
        for n in range(2):
            nc.vector.tensor_copy(cand_planes[n][:], cand_sc[n][:].indirect(lists[1 + n][:]))
        cand_codes = {}

        def gather_cand(n, b):
            cand_codes[n, b] = held("cand_codes%d%d" % (n, b), [P, S], U32)
            nc.vector.tensor_copy(cand_codes[n, b][:], cand_w[n, b][:].bitcast(U32).indirect(lists[1 + n][:]))

        def score_pass(acc, n, b, i):
            cols = slice(i * P, (i + 1) * P)
            nc.tensor.matmul_mx(
                out=acc[:],
                lhsT=cand_codes[n, b][:, cols].bitcast(FP8X4),
                lhsT_scale=cand_planes[n][CAND_ROW[n] + 4 * b :, cols],
                rhs=h_codes[b][:].bitcast(FP8X4),
                rhs_scale=h_sc[b][:],
                start=(b == 0),
                stop=(b == R_PASSES - 1),
            )

        e2 = [bank(PACK + i, "e2%d" % i) for i in range(M_TILES)]
        e3 = [bank(i, "e3%d" % i) for i in range(M_TILES)]
        for b in range(R_PASSES):
            for n, acc in enumerate((e2, e3)):
                gather_cand(n, b)
                for i in range(M_TILES):
                    score_pass(acc[i], n, b, i)
        for i in range(M_TILES):
            nc.vector.tensor_tensor(out=result[:, i, :], in0=e2[i][:], in1=result[:, i, :], op=ALU.min)
            nc.vector.tensor_tensor(out=result[:, i, :], in0=e3[i][:], in1=result[:, i, :], op=ALU.add)
            nc.sync.dma_start(out=out[i * P : (i + 1) * P, :], in_=result[:, i, :])
